import numpy as np
import ml_dtypes


def mxq(x, axis, fmt="e4m3"):
    dtype, down = {"e4m3": (ml_dtypes.float8_e4m3fn, 7), "e5m2": (ml_dtypes.float8_e5m2, 14)}[fmt]
    v = np.moveaxis(np.asarray(x, np.float32).astype(ml_dtypes.bfloat16).astype(np.float64), axis, -1)
    blocks = v.reshape(v.shape[:-1] + (-1, 32))
    amax = np.abs(blocks).max(-1, keepdims=True)
    byte = np.maximum(np.where(amax > 0, np.frexp(amax)[1] - 1 + 127, 0) - down, 1)
    scale = np.exp2(byte - 127.0)
    codes = (blocks / scale).astype(np.float32).astype(dtype).astype(np.float64)
    return np.moveaxis((codes * scale).reshape(v.shape), -1, axis)


WIDE = False


def mx_kscale(k):
    if not WIDE:
        return np.ones(k)
    levels = np.array([10, -10, 5, -5, 0])
    if k % 512:
        return np.exp2(np.random.permutation(np.resize(levels, k // 32))).repeat(32)
    a = np.empty((k // 512, 16))
    for p in range(k // 512):
        a[p, :8] = np.random.permutation(np.resize(levels, 8))
        for g in range(8):
            far = levels[np.abs(levels - a[p, g]) >= 10]
            a[p, g + 8] = far[np.random.randint(len(far))]
    return np.exp2(a.ravel()).repeat(32)


def f64(x):
    return np.asarray(x).astype(np.float64)


def striped(idx):
    return np.tile(idx.reshape(-1, 16).T, (8, 1)).astype(np.uint16)


def unstriped(offs):
    return offs[:16].T.reshape(-1).astype(np.int64)


E2M1 = np.array([0.0, 0.5, 1.0, 1.5, 2.0, 3.0, 4.0, 6.0, -0.0, -0.5, -1.0, -1.5, -2.0, -3.0, -4.0, -6.0])


def pack_weight(w, fmt):
    k, n = w.shape
    w = f64(np.asarray(w, np.float32).astype(ml_dtypes.bfloat16)).reshape(k // 32, 32, n)
    amax = np.abs(w).max(1)
    if fmt == "e4m3":
        byte = np.frexp(amax)[1] - 1 + 127 - 7
    else:
        mant, ex = np.frexp(amax / 6.0)
        byte = np.where(mant > 0.5, ex, ex - 1) + 127
    byte = np.clip(np.where(amax > 0, byte, 1), 1, 254)
    scaled = (w * np.exp2(127.0 - byte)[:, None, :]).reshape(k, n).astype(np.float32)
    by_word = np.ascontiguousarray(scaled.reshape(k // 512, 128, 4, n).transpose(0, 1, 3, 2))
    if fmt == "e4m3":
        words = by_word.astype(ml_dtypes.float8_e4m3fn).view(np.uint8)
    else:
        c = by_word.astype(ml_dtypes.float4_e2m1fn).view(np.uint8) & 0xF
        words = (c[..., 0::2] | (c[..., 1::2] << 4)).reshape(k // 512, 128, 2 * n)
    return np.ascontiguousarray(words), np.ascontiguousarray(byte.astype(np.uint8).reshape(k // 512, 16, n))


def unpack_weight(words, scales, fmt):
    g, _, n = scales.shape
    words = np.ascontiguousarray(words).reshape(g, 128, n, -1)
    if fmt == "e4m3":
        vals = words.view(ml_dtypes.float8_e4m3fn).astype(np.float64)
    else:
        nib = np.empty((g, 128, n, 4), np.uint8)
        nib[..., 0::2] = words & 0xF
        nib[..., 1::2] = words >> 4
        vals = E2M1[nib]
    vals = vals * np.repeat(np.exp2(scales.astype(np.float64) - 127.0), 8, axis=1)[..., None]
    return vals.transpose(0, 1, 3, 2).reshape(g * 512, n)


def gelu(v):
    return 0.5 * v * (1.0 + np.tanh(np.sqrt(2.0 / np.pi) * (v + 0.044715 * v**3)))


def bf(x):
    return np.asarray(x, np.float32).astype(ml_dtypes.bfloat16)


def planes(Y):
    n, m = Y.shape
    b = f64(bf(Y)).reshape(n // 32, 32, m)
    amax = np.abs(b).max(1)
    byte = np.clip(np.where(amax > 0, np.frexp(amax)[1] - 1 + 127 - 7, 1), 1, 254)
    codes = (b * np.exp2(127.0 - byte)[:, None, :]).reshape(n, m).astype(np.float32).astype(ml_dtypes.float8_e4m3fn).view(np.uint8)
    words = codes.reshape(n // 512, 128, 4, m).transpose(0, 1, 3, 2)
    return np.ascontiguousarray(words), np.ascontiguousarray(byte.astype(np.uint8).reshape(n // 512, 16, m))


K, R, H, T, S, T2, P = 1024, 512, 1536, 2048, 512, 1024, 512

def setup_inputs():
    n = np.random.standard_normal
    s = mx_kscale(K)[:, None]
    u = mx_kscale(H)[:, None]
    d = {}
    d["tab_words"], d["tab_scales"] = pack_weight(n((K, T)) * s, "e4m3")
    d["offs"] = striped(np.random.permutation(T)[:S])
    d["w1"] = (0.62 * n((K, R)) / K ** 0.5 / s).astype(np.float32)
    d["w2_words"], d["w2_scales"] = pack_weight(1.5 * n((K, R)) / K ** 0.5 / s, "e2m1")
    d["w3"] = (n((K, R)) / K ** 0.5 / s).astype(np.float32)
    bank = np.repeat([2.4, 1.3, 1.0], R)
    d["page0"] = (n((H, T2)) / bank[:, None]).astype(np.float32)
    d["wgs"] = np.exp(0.3 * n((128, S))).astype(np.float32)
    d["offs2"] = striped(np.random.permutation(T2)[:S])
    d["offs3"] = striped(np.random.permutation(T2)[:P])
    d["gx"] = (bank * np.exp(0.3 * n(H)) * u[:, 0]).astype(np.float32)
    core = 1.8 * n((H, H)) / H ** 0.5
    dim = -2.6 + 1.9 * np.sin(np.arange(H) / 60.0) + 0.8 * n(H)
    d["w4_words"], d["w4_scales"] = pack_weight((core - core.mean(axis=0) + dim / (0.9 * H)) / u, "e4m3")
    d["offs4"] = striped(np.random.permutation(T2)[:P])
    d["gv"] = (0.5 * bank * np.exp(0.3 * n(H))).astype(np.float32)
    return d

def reference(tab_words, tab_scales, offs, w1, w2_words, w2_scales, w3, page0, wgs, offs2, offs3, gx, w4_words, w4_scales, offs4, gv):
    v = unpack_weight(tab_words, tab_scales, "e4m3")[:, unstriped(offs)]
    h1 = np.sin(mxq(f64(w1), 0, "e4m3").T @ v)
    h2 = np.tanh(unpack_weight(w2_words, w2_scales, "e2m1").T @ v)
    h3 = mxq(f64(w3), 0, "e4m3").T @ v
    h = np.concatenate([h1, h2, h3], axis=0)
    page = f64(page0).copy()
    page[:, unstriped(offs2)] = np.tile(f64(wgs), (H // 128, 1)) * h
    x = np.abs(f64(gx)[:, None] * page[:, unstriped(offs3)])
    e = unpack_weight(w4_words, w4_scales, "e4m3").T @ mxq(x, 0, "e4m3")
    total = e + f64(gv)[:, None] * page[:, unstriped(offs4)]
    y = 1.0 / (1.0 + np.exp(-total))
    words, scales = planes(y)
    return y, words, scales

@@ -1,0 +1,274 @@
+import math
+from contextlib import ExitStack
+
+import concourse.mybir as mybir
+
+K, R, H, T, S, T2, M = 1024, 512, 1536, 2048, 512, 1024, 512
+FLOPS = 2 * 3 * K * R * S + 2 * H * H * M
+
+F32 = mybir.dt.float32
+BF16 = mybir.dt.bfloat16
+I32 = mybir.dt.int32
+U32 = mybir.dt.uint32
+U16 = mybir.dt.uint16
+U8 = mybir.dt.uint8
+E4M3 = mybir.dt.float8_e4m3fn_x4
+E2M1 = mybir.dt.float4_e2m1fn_x4
+ACT = mybir.ActivationFunctionType
+ALU = mybir.AluOpType
+
+P = 128
+PACK = 4
+GROUP = P * PACK
+QUADS = 4
+SIN, TANH, LIN = 0, 1, 2
+BANK_ORDER = (TANH, SIN, LIN)
+
+
+def tile_list_dome_seam_page_kernel(tc, tab_words, tab_scales, offs, w1, w2_words, w2_scales, w3, page0, wgs,
+                                              offs2, offs3, gx, w4_words, w4_scales, offs4, gv, out_0, out_1, out_2):
+    nc = tc.nc
+    with ExitStack() as ctx:
+        lists = ctx.enter_context(tc.tile_pool(name="lists", bufs=1))
+        sb = ctx.enter_context(tc.tile_pool(name="sb", bufs=1))
+        psum = ctx.enter_context(tc.psum_pool(name="psum", bufs=1))
+
+        def tile(shape, dtype, name, tag=None, bufs=1):
+            return sb.tile(shape, dtype, name=name, tag=tag or name, bufs=bufs, align_bytes=64)
+
+        def load_list(src, name):
+            t = lists.tile([P, S // 16], U16, name=name)
+            nc.sync.dma_start(t[:], src)
+            return t
+
+        def load_page(bank, t):
+            pg = tile([P, T2], F32, "page_%d_%d" % (bank, t))
+            rows = page0[bank * GROUP:(bank + 1) * GROUP, :].rearrange("(p t) c -> p t c", t=PACK)
+            nc.sync.dma_start(out=pg[:], in_=rows[:, t, :])
+            return pg
+
+        def load_scale_rows(engine, dst, src):
+            for q in range(QUADS):
+                engine.dma_start(out=dst[32 * q:32 * q + 4, :, :].bitcast(I32),
+                                 in_=src[:, 4 * q:4 * q + 4, :].rearrange("a q c -> q a c").bitcast(I32))
+
+        def load_weight(w, a, name):
+            raw = tile([P, PACK, R], F32, name, tag="stage", bufs=2)
+            nc.sync.dma_start(out=raw[:], in_=w[a * GROUP:(a + 1) * GROUP, :].rearrange("(p j) c -> p j c", j=PACK))
+            return raw
+
+        def round_weight(raw, name, tag, bufs):
+            wb = tile([P, R * PACK], BF16, name, tag=tag, bufs=bufs)
+            nc.scalar.copy(out=wb[:].rearrange("p (t m j) -> p m t j", t=PACK, j=PACK),
+                           in_=raw[:].rearrange("p j (m t) -> p m t j", t=PACK))
+            return wb
+
+        def quantize(src, codes, scales):
+            nc.vector.quantize_mx(out=codes.bitcast(E4M3), scales=scales, in_=src)
+
+        def interleave(engine_copy, dst, src):
+            engine_copy(out=dst[:].rearrange("p (c i t) -> p c t i", i=4, t=PACK),
+                        in_=src[:].rearrange("p t (c i) -> p c t i", i=4))
+
+        tab_s = tile([P, 2, T], U8, "tab_s")
+        nc.vector.memset(tab_s[:].rearrange("p a c -> p (a c)").bitcast(I32), 0)
+        w2s_raw = tile([P, 2, R], U8, "w2s_raw")
+        nc.gpsimd.memset(w2s_raw[:].rearrange("p a c -> p (a c)").bitcast(I32), 0)
+        load_scale_rows(nc.gpsimd, w2s_raw, w2_scales)
+        w4s_raw = tile([P, H], U8, "w4s_raw")
+        nc.gpsimd.memset(w4s_raw[:].bitcast(I32), 0)
+        one = tile([P, 1], F32, "one")
+        nc.gpsimd.memset(one[:], 1.0)
+        eighth_pi = tile([P, 1], F32, "eighth_pi")
+        nc.gpsimd.tensor_scalar(eighth_pi[:], one[:], math.pi / 8, 0.0, ALU.mult, ALU.add)
+
+        tab_w = [tile([P, T], U32, "tab_w%d" % a) for a in range(2)]
+        nc.sync.dma_start(out=tab_w[0][:].bitcast(I32), in_=tab_words[0].rearrange("p c i -> p (c i)").bitcast(I32))
+        idx = load_list(offs, "idx")
+        load_scale_rows(nc.sync, tab_s, tab_scales)
+        nc.sync.dma_start(out=tab_w[1][:].bitcast(I32), in_=tab_words[1].rearrange("p c i -> p (c i)").bitcast(I32))
+        w2_raw = tile([P, 2, 2 * R], U8, "w2_raw")
+        nc.sync.dma_start(out=w2_raw[:].bitcast(I32), in_=w2_words.rearrange("a p c -> p a c").bitcast(I32))
+        idx2 = load_list(offs2, "idx2")
+        wgs_rows = wgs.rearrange("(q t) j -> q t j", t=PACK)
+        wgs_first = tile([P, S], F32, "wgs_first")
+        for q in range(QUADS):
+            nc.sync.dma_start(out=wgs_first[32 * q:32 * q + 32, :], in_=wgs_rows[:, 0, :])
+        pages = {}
+        pages[TANH, 0] = load_page(TANH, 0)
+        pages[TANH, 1] = load_page(TANH, 1)
+        wgs_rest = tile([P, PACK - 1, S], F32, "wgs_rest")
+        for q in range(QUADS):
+            nc.sync.dma_start(out=wgs_rest[32 * q:32 * q + 32, :, :], in_=wgs_rows[:, 1:PACK, :])
+        wgs_of = [wgs_first[:]] + [wgs_rest[:, t, :] for t in range(PACK - 1)]
+        w1_raw0 = load_weight(w1, 0, "w1_raw0")
+        pages[TANH, 2] = load_page(TANH, 2)
+        w1_raw1 = load_weight(w1, 1, "w1_raw1")
+        pages[TANH, 3] = load_page(TANH, 3)
+        idx3 = load_list(offs3, "idx3")
+        gx_t = tile([P, 3, PACK], F32, "gx_t")
+        nc.sync.dma_start(out=gx_t[:], in_=gx.rearrange("(a p t) -> p a t", a=3, t=PACK))
+        for t in range(PACK):
+            pages[SIN, t] = load_page(SIN, t)
+
+        v_w = tile([P, 2, S], U32, "v_w")
+        v_s = tile([P, 2, S], U8, "v_s")
+        nc.vector.tensor_copy(v_w[:, 0, :], tab_w[0][:].indirect(idx[:]))
+        for a in range(2):
+            nc.vector.tensor_copy(v_s[:, a, :], tab_s[:, a, :].indirect(idx[:]))
+        w2_s = tile([P, 2, R], U8, "w2_s")
+        nc.vector.tensor_copy(out=w2_s[:].rearrange("p a (t m) -> p a t m", t=PACK),
+                              in_=w2s_raw[:].rearrange("p a (m t) -> p a t m", t=PACK))
+        nc.vector.tensor_copy(v_w[:, 1, :], tab_w[1][:].indirect(idx[:]))
+        w2_w = tile([P, 2, 2 * R], U8, "w2_w")
+        nc.scalar.copy(out=w2_w[:].bitcast(U16).rearrange("p a (t m) -> p a t m", t=PACK),
+                       in_=w2_raw[:].bitcast(U16).rearrange("p a (m t) -> p a t m", t=PACK))
+
+        def first_product(slot, codes_of, scales_of):
+            acc = psum.tile([P, S], F32, name="h_acc%d" % slot, tag="bank%d" % (slot % 4))
+            for a in range(2):
+                nc.tensor.matmul_mx(out=acc[:], lhsT=codes_of(a), lhsT_scale=scales_of(a),
+                                    rhs=v_w[:, a, :].bitcast(E4M3), rhs_scale=v_s[:, a, :],
+                                    start=(a == 0), stop=(a == 1))
+            return acc
+
+        def scatter(bank, t, h):
+            nc.vector.tensor_tensor(pages[bank, t][:].indirect(idx2[:]), h[:, t, :], wgs_of[t], ALU.mult)
+
+        def pick_overlap(bank, t, picked):
+            nc.vector.tensor_copy(picked[:, t, :], pages[bank, t][:].indirect(idx3[:]))
+
+        x_w = [tile([P, M], U32, "x_w%d" % a) for a in range(3)]
+        x_s = [tile([P, M], U8, "x_s%d" % a) for a in range(3)]
+
+        def round_x(bank, picked):
+            xb = tile([P, PACK, M], BF16, "xb%d" % bank, tag="xb")
+            for t in range(PACK):
+                nc.scalar.activation(out=xb[:, t, :], in_=picked[:, t, :], func=ACT.Abs, scale=gx_t[:, bank, t:t + 1])
+            xi = tile([P, M * PACK], BF16, "xi%d" % bank, tag="woven", bufs=3)
+            interleave(nc.scalar.copy, xi, xb)
+            return xi
+
+        h_tanh = tile([P, PACK, S], F32, "h_tanh", tag="h_a")
+        for t in range(PACK):
+            acc = first_product(t, lambda a: w2_w[:, a, 2 * P * t:2 * P * (t + 1)].bitcast(E2M1),
+                                lambda a: w2_s[:, a, P * t:P * (t + 1)])
+            nc.scalar.activation(out=h_tanh[:, t, :], in_=acc[:], func=ACT.Tanh)
+        w1_b0 = round_weight(w1_raw0, "w1_b0", "woven", 3)
+        w1_b1 = round_weight(w1_raw1, "w1_b1", "picked", 1)
+        w3_raw0 = load_weight(w3, 0, "w3_raw0")
+        w3_raw1 = load_weight(w3, 1, "w3_raw1")
+        for q in range(QUADS):
+            nc.sync.dma_start(out=w4s_raw[32 * q:32 * q + 12, :].bitcast(I32),
+                              in_=w4_scales[:, 4 * q:4 * q + 4, :].bitcast(I32))
+        for t in range(PACK):
+            pages[LIN, t] = load_page(LIN, t)
+        w4_raw = [tile([P, H], U32, "w4_raw%d" % a) for a in range(3)]
+        for a in BANK_ORDER:
+            nc.sync.dma_start(out=w4_raw[a][:].bitcast(I32), in_=w4_words[a].rearrange("p c i -> p (c i)").bitcast(I32))
+        idx4 = load_list(offs4, "idx4")
+        gv_t = tile([P, 3, PACK], F32, "gv_t")
+        nc.sync.dma_start(out=gv_t[:], in_=gv.rearrange("(a p t) -> p a t", a=3, t=PACK))
+
+        for t in range(PACK):
+            scatter(TANH, t, h_tanh)
+        w1_w = tile([P, 2, R], U32, "w1_w")
+        w1_s = tile([P, 2, R], U8, "w1_s")
+        quantize(w1_b0[:], w1_w[:, 0, :], w1_s[:, 0, :])
+        quantize(w1_b1[:], w1_w[:, 1, :], w1_s[:, 1, :])
+        picked = tile([P, PACK, M], F32, "picked_tanh", tag="picked")
+        for t in range(PACK):
+            pick_overlap(TANH, t, picked)
+
+        h_sin = tile([P, PACK, S], F32, "h_sin", tag="h_b")
+        sin_work = tile([P, 2, S], F32, "sin_work", tag="xb")
+        for t in range(PACK):
+            acc = first_product(4 + t, lambda a: w1_w[:, a, P * t:P * (t + 1)].bitcast(E4M3),
+                                lambda a: w1_s[:, a, P * t:P * (t + 1)])
+            work = sin_work[:, t, :] if t < 2 else h_sin[:, t, :]
+            nc.scalar.activation(out=work, in_=acc[:], func=ACT.Sin, scale=0.25, bias=eighth_pi[:])
+            nc.scalar.activation(out=work, in_=work, func=ACT.Square)
+            nc.scalar.activation(out=work, in_=work, func=ACT.Square, scale=-2.0, bias=one[:])
+            nc.scalar.activation(out=h_sin[:, t, :], in_=work, func=ACT.Identity, scale=-2.0, bias=one[:])
+        xi_tanh = round_x(TANH, picked)
+        w3_b0 = round_weight(w3_raw0, "w3_b0", "woven", 3)
+        w3_b1 = round_weight(w3_raw1, "w3_b1", "picked", 1)
+        for t in range(PACK):
+            scatter(SIN, t, h_sin)
+        quantize(xi_tanh[:], x_w[TANH][:], x_s[TANH][:])
+        w4_s = tile([P, H], U8, "w4_s")
+        nc.vector.tensor_copy(out=w4_s[:].rearrange("p (g t m) -> p g t m", g=3, t=PACK),
+                              in_=w4s_raw[:].rearrange("p (g m t) -> p g t m", g=3, t=PACK))
+        w3_w = tile([P, 2, R], U32, "w3_w")
+        w3_s = tile([P, 2, R], U8, "w3_s")
+        quantize(w3_b0[:], w3_w[:, 0, :], w3_s[:, 0, :])
+        quantize(w3_b1[:], w3_w[:, 1, :], w3_s[:, 1, :])
+        picked = tile([P, PACK, M], F32, "picked_sin", tag="picked")
+        for t in range(PACK):
+            pick_overlap(SIN, t, picked)
+
+        h_lin = tile([P, PACK, S], F32, "h_lin", tag="h_a")
+        for t in range(PACK):
+            acc = first_product(8 + t, lambda a: w3_w[:, a, P * t:P * (t + 1)].bitcast(E4M3),
+                                lambda a: w3_s[:, a, P * t:P * (t + 1)])
+            nc.scalar.copy(out=h_lin[:, t, :], in_=acc[:])
+        xi_sin = round_x(SIN, picked)
+        w4_w = [tile([P, H], U32, "w4_w%d" % a) for a in range(3)]
+        for a in BANK_ORDER:
+            nc.scalar.copy(out=w4_w[a][:].rearrange("p (g t c i) -> p g c t i", g=3, t=PACK, i=4),
+                           in_=w4_raw[a][:].rearrange("p (g c i t) -> p g c t i", g=3, t=PACK, i=4))
+        picked = tile([P, PACK, M], F32, "picked_lin", tag="picked")
+        scatter(LIN, 0, h_lin)
+        for t in range(1, PACK):
+            scatter(LIN, t, h_lin)
+            pick_overlap(LIN, t - 1, picked)
+        quantize(xi_sin[:], x_w[SIN][:], x_s[SIN][:])
+        pick_overlap(LIN, PACK - 1, picked)
+        xi_lin = round_x(LIN, picked)
+
+        opposite = tile([P, PACK, M], F32, "opposite", tag="h_a")
+
+        def pick_opposite(n):
+            nc.vector.tensor_copy(opposite[:, n % PACK, :], pages[n // PACK, n % PACK][:].indirect(idx4[:]))
+
+        for n in range(PACK):
+            pick_opposite(n)
+        quantize(xi_lin[:], x_w[LIN][:], x_s[LIN][:])
+
+        y_w = [tile([P, M], U32, "y_w%d" % g) for g in range(3)]
+        y_s = tile([P, 3, M], U8, "y_s")
+        y_rounded = {}
+
+        def finish_group(g):
+            quantize(y_rounded[g][:], y_w[g][:], y_s[:, g, :])
+            nc.sync.dma_start(out=out_1[g].rearrange("p m t -> p (m t)").bitcast(I32), in_=y_w[g][:].bitcast(I32))
+
+        for g in range(3):
+            if g == 0:
+                y = tile([P, PACK, M], F32, "y0", tag="h_b")
+            else:
+                y = tile([P, PACK, M], F32, "y%d" % g, tag="stage", bufs=2)
+            y_rows = out_0[g * GROUP:(g + 1) * GROUP, :].rearrange("(p t) m -> p t m", t=PACK)
+            for t in range(PACK):
+                n = PACK * g + t
+                acc = psum.tile([P, M], F32, name="e_acc%d" % n, tag="bank%d" % ((4 + n) % 8))
+                cols = slice(P * n, P * (n + 1))
+                for a in BANK_ORDER:
+                    nc.tensor.matmul_mx(out=acc[:], lhsT=w4_w[a][:, cols].bitcast(E4M3), lhsT_scale=w4_s[4 * a:P, cols],
+                                        rhs=x_w[a][:].bitcast(E4M3), rhs_scale=x_s[a][:],
+                                        start=(a == BANK_ORDER[0]), stop=(a == BANK_ORDER[-1]))
+                nc.vector.scalar_tensor_tensor(out=y[:, t, :], in0=opposite[:, t, :], scalar=gv_t[:, g, t:t + 1],
+                                               in1=acc[:], op0=ALU.mult, op1=ALU.add)
+                if 1 <= n and n + 3 < 3 * PACK:
+                    pick_opposite(n + 3)
+                nc.scalar.activation(out=y[:, t, :], in_=y[:, t, :], func=ACT.Sigmoid)
+                nc.sync.dma_start(out=y_rows[:, t, :], in_=y[:, t, :])
+                if g >= 1 and t == 2:
+                    finish_group(g - 1)
+            y_rounded[g] = tile([P, M * PACK], BF16, "y_b%d" % g, tag="woven", bufs=3)
+            interleave(nc.vector.tensor_copy if g == 2 else nc.scalar.copy, y_rounded[g], y)
+        finish_group(2)
+        for q in range(QUADS):
+            engine = nc.sync if q < 2 else nc.scalar
+            engine.dma_start(out=out_2[:, 4 * q:4 * q + 4, :].rearrange("g q m -> q g m").bitcast(I32),
+                             in_=y_s[32 * q:32 * q + 4, :, :].bitcast(I32))

@@ -67,14 +67,14 @@ def tile_list_dome_seam_page_kernel(tc, tab_words, tab_scales, offs, w1, w2_word
             nc.vector.quantize_mx(out=codes.bitcast(E4M3), scales=scales, in_=src)
 
         def interleave(engine_copy, dst, src):
-            engine_copy(out=dst[:].rearrange("p (c i t) -> p c t i", i=4, t=PACK),
-                        in_=src[:].rearrange("p t (c i) -> p c t i", i=4))
+            engine_copy(out=dst.rearrange("p (c i t) -> p c t i", i=4, t=PACK),
+                        in_=src.rearrange("p t (c i) -> p c t i", i=4))
 
         tab_s = tile([P, 2, T], U8, "tab_s")
         nc.vector.memset(tab_s[:].rearrange("p a c -> p (a c)").bitcast(I32), 0)
         w2s_raw = tile([P, 2, R], U8, "w2s_raw")
         nc.gpsimd.memset(w2s_raw[:].rearrange("p a c -> p (a c)").bitcast(I32), 0)
-        load_scale_rows(nc.gpsimd, w2s_raw, w2_scales)
+        load_scale_rows(nc.sync, w2s_raw, w2_scales)
         w4s_raw = tile([P, H], U8, "w4s_raw")
         nc.gpsimd.memset(w4s_raw[:].bitcast(I32), 0)
         one = tile([P, 1], F32, "one")
@@ -86,14 +86,14 @@ def tile_list_dome_seam_page_kernel(tc, tab_words, tab_scales, offs, w1, w2_word
         nc.sync.dma_start(out=tab_w[0][:].bitcast(I32), in_=tab_words[0].rearrange("p c i -> p (c i)").bitcast(I32))
         idx = load_list(offs, "idx")
         load_scale_rows(nc.sync, tab_s, tab_scales)
-        nc.sync.dma_start(out=tab_w[1][:].bitcast(I32), in_=tab_words[1].rearrange("p c i -> p (c i)").bitcast(I32))
         w2_raw = tile([P, 2, 2 * R], U8, "w2_raw")
         nc.sync.dma_start(out=w2_raw[:].bitcast(I32), in_=w2_words.rearrange("a p c -> p a c").bitcast(I32))
+        nc.sync.dma_start(out=tab_w[1][:].bitcast(I32), in_=tab_words[1].rearrange("p c i -> p (c i)").bitcast(I32))
         idx2 = load_list(offs2, "idx2")
         wgs_rows = wgs.rearrange("(q t) j -> q t j", t=PACK)
         wgs_first = tile([P, S], F32, "wgs_first")
         for q in range(QUADS):
-            nc.sync.dma_start(out=wgs_first[32 * q:32 * q + 32, :], in_=wgs_rows[:, 0, :])
+            nc.gpsimd.dma_start(out=wgs_first[32 * q:32 * q + 32, :], in_=wgs_rows[:, 0, :])
         pages = {}
         pages[TANH, 0] = load_page(TANH, 0)
         pages[TANH, 1] = load_page(TANH, 1)
@@ -104,36 +104,40 @@ def tile_list_dome_seam_page_kernel(tc, tab_words, tab_scales, offs, w1, w2_word
         w1_raw0 = load_weight(w1, 0, "w1_raw0")
         pages[TANH, 2] = load_page(TANH, 2)
         w1_raw1 = load_weight(w1, 1, "w1_raw1")
+        pages[SIN, 0] = load_page(SIN, 0)
+        pages[SIN, 1] = load_page(SIN, 1)
         pages[TANH, 3] = load_page(TANH, 3)
         idx3 = load_list(offs3, "idx3")
         gx_t = tile([P, 3, PACK], F32, "gx_t")
         nc.sync.dma_start(out=gx_t[:], in_=gx.rearrange("(a p t) -> p a t", a=3, t=PACK))
-        for t in range(PACK):
+        for t in range(2, PACK):
             pages[SIN, t] = load_page(SIN, t)
 
         v_w = tile([P, 2, S], U32, "v_w")
         v_s = tile([P, 2, S], U8, "v_s")
-        nc.vector.tensor_copy(v_w[:, 0, :], tab_w[0][:].indirect(idx[:]))
-        for a in range(2):
-            nc.vector.tensor_copy(v_s[:, a, :], tab_s[:, a, :].indirect(idx[:]))
         w2_s = tile([P, 2, R], U8, "w2_s")
         nc.vector.tensor_copy(out=w2_s[:].rearrange("p a (t m) -> p a t m", t=PACK),
                               in_=w2s_raw[:].rearrange("p a (m t) -> p a t m", t=PACK))
-        nc.vector.tensor_copy(v_w[:, 1, :], tab_w[1][:].indirect(idx[:]))
+        nc.vector.tensor_copy(v_w[:, 0, :], tab_w[0][:].indirect(idx[:]))
+        for a in range(2):
+            nc.vector.tensor_copy(v_s[:, a, :], tab_s[:, a, :].indirect(idx[:]))
+        for j0 in (0, S // 2):
+            nc.vector.tensor_copy(v_w[:, 1, j0:j0 + S // 2], tab_w[1][:].indirect(idx[:, j0 // 16:(j0 + S // 2) // 16]))
         w2_w = tile([P, 2, 2 * R], U8, "w2_w")
         nc.scalar.copy(out=w2_w[:].bitcast(U16).rearrange("p a (t m) -> p a t m", t=PACK),
                        in_=w2_raw[:].bitcast(U16).rearrange("p a (m t) -> p a t m", t=PACK))
 
-        def first_product(slot, codes_of, scales_of):
-            acc = psum.tile([P, S], F32, name="h_acc%d" % slot, tag="bank%d" % (slot % 4))
+        def first_product(psum_bank, codes_of, scales_of, j0=0, j1=S):
+            acc = psum.tile([P, j1 - j0], F32, name="h_acc", tag="bank%d" % psum_bank)
             for a in range(2):
                 nc.tensor.matmul_mx(out=acc[:], lhsT=codes_of(a), lhsT_scale=scales_of(a),
-                                    rhs=v_w[:, a, :].bitcast(E4M3), rhs_scale=v_s[:, a, :],
+                                    rhs=v_w[:, a, j0:j1].bitcast(E4M3), rhs_scale=v_s[:, a, j0:j1],
                                     start=(a == 0), stop=(a == 1))
             return acc
 
-        def scatter(bank, t, h):
-            nc.vector.tensor_tensor(pages[bank, t][:].indirect(idx2[:]), h[:, t, :], wgs_of[t], ALU.mult)
+        def scatter(bank, t, h, j0=0, j1=S):
+            nc.vector.tensor_tensor(pages[bank, t][:].indirect(idx2[:, j0 // 16:j1 // 16]), h[:, t, j0:j1],
+                                    wgs_of[t][:, j0:j1], ALU.mult)
 
         def pick_overlap(bank, t, picked):
             nc.vector.tensor_copy(picked[:, t, :], pages[bank, t][:].indirect(idx3[:]))
@@ -146,14 +150,15 @@ def tile_list_dome_seam_page_kernel(tc, tab_words, tab_scales, offs, w1, w2_word
             for t in range(PACK):
                 nc.scalar.activation(out=xb[:, t, :], in_=picked[:, t, :], func=ACT.Abs, scale=gx_t[:, bank, t:t + 1])
             xi = tile([P, M * PACK], BF16, "xi%d" % bank, tag="woven", bufs=3)
-            interleave(nc.scalar.copy, xi, xb)
+            interleave(nc.scalar.copy, xi[:], xb[:])
             return xi
 
         h_tanh = tile([P, PACK, S], F32, "h_tanh", tag="h_a")
-        for t in range(PACK):
-            acc = first_product(t, lambda a: w2_w[:, a, 2 * P * t:2 * P * (t + 1)].bitcast(E2M1),
-                                lambda a: w2_s[:, a, P * t:P * (t + 1)])
-            nc.scalar.activation(out=h_tanh[:, t, :], in_=acc[:], func=ACT.Tanh)
+        tanh_parts = [(0, 0, S // 2), (0, S // 2, S)] + [(t, 0, S) for t in range(1, PACK)]
+        for psum_bank, (t, j0, j1) in enumerate(tanh_parts):
+            acc = first_product(psum_bank, lambda a: w2_w[:, a, 2 * P * t:2 * P * (t + 1)].bitcast(E2M1),
+                                lambda a: w2_s[:, a, P * t:P * (t + 1)], j0, j1)
+            nc.scalar.activation(out=h_tanh[:, t, j0:j1], in_=acc[:], func=ACT.Tanh)
         w1_b0 = round_weight(w1_raw0, "w1_b0", "woven", 3)
         w1_b1 = round_weight(w1_raw1, "w1_b1", "picked", 1)
         w3_raw0 = load_weight(w3, 0, "w3_raw0")
@@ -170,12 +175,13 @@ def tile_list_dome_seam_page_kernel(tc, tab_words, tab_scales, offs, w1, w2_word
         gv_t = tile([P, 3, PACK], F32, "gv_t")
         nc.sync.dma_start(out=gv_t[:], in_=gv.rearrange("(a p t) -> p a t", a=3, t=PACK))
 
-        for t in range(PACK):
-            scatter(TANH, t, h_tanh)
+        for t, j0, j1 in tanh_parts[:-1]:
+            scatter(TANH, t, h_tanh, j0, j1)
         w1_w = tile([P, 2, R], U32, "w1_w")
         w1_s = tile([P, 2, R], U8, "w1_s")
         quantize(w1_b0[:], w1_w[:, 0, :], w1_s[:, 0, :])
         quantize(w1_b1[:], w1_w[:, 1, :], w1_s[:, 1, :])
+        scatter(TANH, PACK - 1, h_tanh)
         picked = tile([P, PACK, M], F32, "picked_tanh", tag="picked")
         for t in range(PACK):
             pick_overlap(TANH, t, picked)
@@ -183,7 +189,7 @@ def tile_list_dome_seam_page_kernel(tc, tab_words, tab_scales, offs, w1, w2_word
         h_sin = tile([P, PACK, S], F32, "h_sin", tag="h_b")
         sin_work = tile([P, 2, S], F32, "sin_work", tag="xb")
         for t in range(PACK):
-            acc = first_product(4 + t, lambda a: w1_w[:, a, P * t:P * (t + 1)].bitcast(E4M3),
+            acc = first_product(t, lambda a: w1_w[:, a, P * t:P * (t + 1)].bitcast(E4M3),
                                 lambda a: w1_s[:, a, P * t:P * (t + 1)])
             work = sin_work[:, t, :] if t < 2 else h_sin[:, t, :]
             nc.scalar.activation(out=work, in_=acc[:], func=ACT.Sin, scale=0.25, bias=eighth_pi[:])
@@ -209,7 +215,7 @@ def tile_list_dome_seam_page_kernel(tc, tab_words, tab_scales, offs, w1, w2_word
 
         h_lin = tile([P, PACK, S], F32, "h_lin", tag="h_a")
         for t in range(PACK):
-            acc = first_product(8 + t, lambda a: w3_w[:, a, P * t:P * (t + 1)].bitcast(E4M3),
+            acc = first_product(t, lambda a: w3_w[:, a, P * t:P * (t + 1)].bitcast(E4M3),
                                 lambda a: w3_s[:, a, P * t:P * (t + 1)])
             nc.scalar.copy(out=h_lin[:, t, :], in_=acc[:])
         xi_sin = round_x(SIN, picked)
@@ -219,29 +225,45 @@ def tile_list_dome_seam_page_kernel(tc, tab_words, tab_scales, offs, w1, w2_word
                            in_=w4_raw[a][:].rearrange("p (g c i t) -> p g c t i", g=3, t=PACK, i=4))
         picked = tile([P, PACK, M], F32, "picked_lin", tag="picked")
         scatter(LIN, 0, h_lin)
-        for t in range(1, PACK):
-            scatter(LIN, t, h_lin)
-            pick_overlap(LIN, t - 1, picked)
+        scatter(LIN, 1, h_lin)
+        pick_overlap(LIN, 0, picked)
+        scatter(LIN, 2, h_lin)
+        pick_overlap(LIN, 1, picked)
         quantize(xi_sin[:], x_w[SIN][:], x_s[SIN][:])
-        pick_overlap(LIN, PACK - 1, picked)
-        xi_lin = round_x(LIN, picked)
+        pick_overlap(LIN, 2, picked)
+        scatter(LIN, 3, h_lin)
+        xb = tile([P, PACK - 1, M], BF16, "xb_lin", tag="xb")
+        for t in range(PACK - 1):
+            nc.scalar.activation(out=xb[:, t, :], in_=picked[:, t, :], func=ACT.Abs, scale=gx_t[:, LIN, t:t + 1])
+        xi_lin = tile([P, M * PACK], BF16, "xi_lin", tag="last_x")
+        xi_view = xi_lin[:].rearrange("p (m t) -> p m t", t=PACK)
+        nc.scalar.copy(out=xi_view[:, :, 0:PACK - 1], in_=xb[:].rearrange("p t m -> p m t"))
 
-        opposite = tile([P, PACK, M], F32, "opposite", tag="h_a")
+        opposite = tile([P, PACK - 1, M], F32, "opposite", tag="h_a")
+        slots = [opposite[:, t, :] for t in range(PACK - 1)]
 
         def pick_opposite(n):
-            nc.vector.tensor_copy(opposite[:, n % PACK, :], pages[n // PACK, n % PACK][:].indirect(idx4[:]))
+            nc.vector.tensor_copy(slots[n % PACK], pages[n // PACK, n % PACK][:].indirect(idx4[:]))
 
-        for n in range(PACK):
-            pick_opposite(n)
+        pick_opposite(0)
+        pick_overlap(LIN, PACK - 1, picked)
+        nc.scalar.activation(out=xi_view[:, :, PACK - 1], in_=picked[:, PACK - 1, :], func=ACT.Abs,
+                             scale=gx_t[:, LIN, PACK - 1:PACK])
+        pick_opposite(1)
+        pick_opposite(2)
         quantize(xi_lin[:], x_w[LIN][:], x_s[LIN][:])
+        opposite_late = tile([P, M], F32, "opposite_late", tag="last_x")
+        slots.append(opposite_late[:])
+        pick_opposite(3)
 
         y_w = [tile([P, M], U32, "y_w%d" % g) for g in range(3)]
         y_s = tile([P, 3, M], U8, "y_s")
         y_rounded = {}
 
-        def finish_group(g):
-            quantize(y_rounded[g][:], y_w[g][:], y_s[:, g, :])
-            nc.sync.dma_start(out=out_1[g].rearrange("p m t -> p (m t)").bitcast(I32), in_=y_w[g][:].bitcast(I32))
+        def finish_group(g, m0, m1):
+            quantize(y_rounded[g][:, PACK * m0:PACK * m1], y_w[g][:, m0:m1], y_s[:, g, m0:m1])
+            nc.sync.dma_start(out=out_1[g].rearrange("p m t -> p (m t)").bitcast(I32)[:, m0:m1],
+                              in_=y_w[g][:, m0:m1].bitcast(I32))
 
         for g in range(3):
             if g == 0:
@@ -257,17 +279,26 @@ def tile_list_dome_seam_page_kernel(tc, tab_words, tab_scales, offs, w1, w2_word
                     nc.tensor.matmul_mx(out=acc[:], lhsT=w4_w[a][:, cols].bitcast(E4M3), lhsT_scale=w4_s[4 * a:P, cols],
                                         rhs=x_w[a][:].bitcast(E4M3), rhs_scale=x_s[a][:],
                                         start=(a == BANK_ORDER[0]), stop=(a == BANK_ORDER[-1]))
-                nc.vector.scalar_tensor_tensor(out=y[:, t, :], in0=opposite[:, t, :], scalar=gv_t[:, g, t:t + 1],
-                                               in1=acc[:], op0=ALU.mult, op1=ALU.add)
+                halves = [slice(0, M // 2), slice(M // 2, M)] if n == 3 * PACK - 1 else [slice(0, M)]
+                for part in halves:
+                    nc.vector.scalar_tensor_tensor(out=y[:, t, part], in0=slots[t][:, part], scalar=gv_t[:, g, t:t + 1],
+                                                   in1=acc[:, part], op0=ALU.mult, op1=ALU.add)
                 if 1 <= n and n + 3 < 3 * PACK:
                     pick_opposite(n + 3)
-                nc.scalar.activation(out=y[:, t, :], in_=y[:, t, :], func=ACT.Sigmoid)
+                for part in halves:
+                    nc.scalar.activation(out=y[:, t, part], in_=y[:, t, part], func=ACT.Sigmoid)
                 nc.sync.dma_start(out=y_rows[:, t, :], in_=y[:, t, :])
-                if g >= 1 and t == 2:
-                    finish_group(g - 1)
+                if (g, t) in ((1, 2), (2, 3)):
+                    finish_group(g - 1, 0, M)
             y_rounded[g] = tile([P, M * PACK], BF16, "y_b%d" % g, tag="woven", bufs=3)
-            interleave(nc.vector.tensor_copy if g == 2 else nc.scalar.copy, y_rounded[g], y)
-        finish_group(2)
+            if g < 2:
+                interleave(nc.scalar.copy, y_rounded[g][:], y[:])
+            else:
+                for m0 in (0, M // 2):
+                    m1 = m0 + M // 2
+                    interleave(nc.vector.tensor_copy, y_rounded[g][:, PACK * m0:PACK * m1], y[:, :, m0:m1])
+                for m0 in (0, M // 2):
+                    finish_group(g, m0, m0 + M // 2)
         for q in range(QUADS):
             engine = nc.sync if q < 2 else nc.scalar
             engine.dma_start(out=out_2[:, 4 * q:4 * q + 4, :].rearrange("g q m -> q g m").bitcast(I32),

@@ -22,7 +22,7 @@ PACK = 4
 GROUP = P * PACK
 QUADS = 4
 SIN, TANH, LIN = 0, 1, 2
-BANK_ORDER = (TANH, SIN, LIN)
+BANK_ORDER = (TANH, LIN, SIN)
 
 
 def tile_list_dome_seam_page_kernel(tc, tab_words, tab_scales, offs, w1, w2_words, w2_scales, w3, page0, wgs,
@@ -53,7 +53,7 @@ def tile_list_dome_seam_page_kernel(tc, tab_words, tab_scales, offs, w1, w2_word
                                  in_=src[:, 4 * q:4 * q + 4, :].rearrange("a q c -> q a c").bitcast(I32))
 
         def load_weight(w, a, name):
-            raw = tile([P, PACK, R], F32, name, tag="stage", bufs=2)
+            raw = tile([P, PACK, R], F32, name, tag="stage", bufs=3)
             nc.sync.dma_start(out=raw[:], in_=w[a * GROUP:(a + 1) * GROUP, :].rearrange("(p j) c -> p j c", j=PACK))
             return raw
 
@@ -101,17 +101,15 @@ def tile_list_dome_seam_page_kernel(tc, tab_words, tab_scales, offs, w1, w2_word
         for q in range(QUADS):
             nc.sync.dma_start(out=wgs_rest[32 * q:32 * q + 32, :, :], in_=wgs_rows[:, 1:PACK, :])
         wgs_of = [wgs_first[:]] + [wgs_rest[:, t, :] for t in range(PACK - 1)]
-        w1_raw0 = load_weight(w1, 0, "w1_raw0")
         pages[TANH, 2] = load_page(TANH, 2)
-        w1_raw1 = load_weight(w1, 1, "w1_raw1")
-        pages[SIN, 0] = load_page(SIN, 0)
-        pages[SIN, 1] = load_page(SIN, 1)
+        w3_raw0 = load_weight(w3, 0, "w3_raw0")
         pages[TANH, 3] = load_page(TANH, 3)
+        w3_raw1 = load_weight(w3, 1, "w3_raw1")
         idx3 = load_list(offs3, "idx3")
         gx_t = tile([P, 3, PACK], F32, "gx_t")
         nc.sync.dma_start(out=gx_t[:], in_=gx.rearrange("(a p t) -> p a t", a=3, t=PACK))
-        for t in range(2, PACK):
-            pages[SIN, t] = load_page(SIN, t)
+        w1_raw0 = load_weight(w1, 0, "w1_raw0")
+        pages[LIN, 0] = load_page(LIN, 0)
 
         v_w = tile([P, 2, S], U32, "v_w")
         v_s = tile([P, 2, S], U8, "v_s")
@@ -140,7 +138,7 @@ def tile_list_dome_seam_page_kernel(tc, tab_words, tab_scales, offs, w1, w2_word
                                     wgs_of[t][:, j0:j1], ALU.mult)
 
         def pick_overlap(bank, t, picked):
-            nc.vector.tensor_copy(picked[:, t, :], pages[bank, t][:].indirect(idx3[:]))
+            nc.vector.tensor_copy(picked, pages[bank, t][:].indirect(idx3[:]))
 
         x_w = [tile([P, M], U32, "x_w%d" % a) for a in range(3)]
         x_s = [tile([P, M], U8, "x_s%d" % a) for a in range(3)]
@@ -148,7 +146,10 @@ def tile_list_dome_seam_page_kernel(tc, tab_words, tab_scales, offs, w1, w2_word
         def round_x(bank, picked):
             xb = tile([P, PACK, M], BF16, "xb%d" % bank, tag="xb")
             for t in range(PACK):
-                nc.scalar.activation(out=xb[:, t, :], in_=picked[:, t, :], func=ACT.Abs, scale=gx_t[:, bank, t:t + 1])
+                nc.scalar.activation(out=xb[:, t, :], in_=picked[t], func=ACT.Abs, scale=gx_t[:, bank, t:t + 1])
+            return xb
+
+        def weave_x(bank, xb):
             xi = tile([P, M * PACK], BF16, "xi%d" % bank, tag="woven", bufs=3)
             interleave(nc.scalar.copy, xi[:], xb[:])
             return xi
@@ -159,34 +160,68 @@ def tile_list_dome_seam_page_kernel(tc, tab_words, tab_scales, offs, w1, w2_word
             acc = first_product(psum_bank, lambda a: w2_w[:, a, 2 * P * t:2 * P * (t + 1)].bitcast(E2M1),
                                 lambda a: w2_s[:, a, P * t:P * (t + 1)], j0, j1)
             nc.scalar.activation(out=h_tanh[:, t, j0:j1], in_=acc[:], func=ACT.Tanh)
-        w1_b0 = round_weight(w1_raw0, "w1_b0", "woven", 3)
-        w1_b1 = round_weight(w1_raw1, "w1_b1", "picked", 1)
-        w3_raw0 = load_weight(w3, 0, "w3_raw0")
-        w3_raw1 = load_weight(w3, 1, "w3_raw1")
+        w3_b0 = round_weight(w3_raw0, "w3_b0", "woven", 3)
+        w3_b1 = round_weight(w3_raw1, "w3_b1", "picked", 1)
+        w1_raw1 = load_weight(w1, 1, "w1_raw1")
+        pages[LIN, 1] = load_page(LIN, 1)
+        pages[LIN, 2] = load_page(LIN, 2)
         for q in range(QUADS):
             nc.sync.dma_start(out=w4s_raw[32 * q:32 * q + 12, :].bitcast(I32),
                               in_=w4_scales[:, 4 * q:4 * q + 4, :].bitcast(I32))
+        pages[LIN, PACK - 1] = load_page(LIN, PACK - 1)
         for t in range(PACK):
-            pages[LIN, t] = load_page(LIN, t)
+            pages[SIN, t] = load_page(SIN, t)
         w4_raw = [tile([P, H], U32, "w4_raw%d" % a) for a in range(3)]
-        for a in BANK_ORDER:
+
+        def load_w4(a):
             nc.sync.dma_start(out=w4_raw[a][:].bitcast(I32), in_=w4_words[a].rearrange("p c i -> p (c i)").bitcast(I32))
+
+        load_w4(TANH)
+        load_w4(LIN)
+        load_w4(SIN)
         idx4 = load_list(offs4, "idx4")
         gv_t = tile([P, 3, PACK], F32, "gv_t")
         nc.sync.dma_start(out=gv_t[:], in_=gv.rearrange("(a p t) -> p a t", a=3, t=PACK))
 
-        for t, j0, j1 in tanh_parts[:-1]:
+        for t, j0, j1 in tanh_parts:
             scatter(TANH, t, h_tanh, j0, j1)
+        picked_early = tile([P, 2, M], F32, "picked_tanh_early", tag="h_a")
+        for t in range(2):
+            pick_overlap(TANH, t, picked_early[:, t, :])
+        w3_w = tile([P, 2, R], U32, "w3_w")
+        w3_s = tile([P, 2, R], U8, "w3_s")
+        quantize(w3_b0[:], w3_w[:, 0, :], w3_s[:, 0, :])
+        quantize(w3_b1[:], w3_w[:, 1, :], w3_s[:, 1, :])
+        picked_late = tile([P, 2, M], F32, "picked_tanh_late", tag="picked")
+        picked = [picked_early[:, 0, :], picked_early[:, 1, :], picked_late[:, 0, :], picked_late[:, 1, :]]
+        for t in range(2, PACK):
+            pick_overlap(TANH, t, picked[t])
+
+        h_lin = tile([P, PACK, S], F32, "h_lin", tag="h_b")
+        for t in range(PACK):
+            acc = first_product(t, lambda a: w3_w[:, a, P * t:P * (t + 1)].bitcast(E4M3),
+                                lambda a: w3_s[:, a, P * t:P * (t + 1)])
+            nc.scalar.copy(out=h_lin[:, t, :], in_=acc[:])
+        w1_b0 = round_weight(w1_raw0, "w1_b0", "woven", 3)
+        xb_tanh = round_x(TANH, picked)
+        w1_b1 = round_weight(w1_raw1, "w1_b1", "picked", 1)
+        xi_tanh = weave_x(TANH, xb_tanh)
+        for t in range(PACK):
+            scatter(LIN, t, h_lin)
         w1_w = tile([P, 2, R], U32, "w1_w")
         w1_s = tile([P, 2, R], U8, "w1_s")
         quantize(w1_b0[:], w1_w[:, 0, :], w1_s[:, 0, :])
         quantize(w1_b1[:], w1_w[:, 1, :], w1_s[:, 1, :])
-        scatter(TANH, PACK - 1, h_tanh)
-        picked = tile([P, PACK, M], F32, "picked_tanh", tag="picked")
+        quantize(xi_tanh[:], x_w[TANH][:], x_s[TANH][:])
+        w4_s = tile([P, H], U8, "w4_s")
+        nc.vector.tensor_copy(out=w4_s[:].rearrange("p (g t m) -> p g t m", g=3, t=PACK),
+                              in_=w4s_raw[:].rearrange("p (g m t) -> p g t m", g=3, t=PACK))
+        picked_lin = tile([P, PACK, M], F32, "picked_lin", tag="picked")
+        picked = [picked_lin[:, t, :] for t in range(PACK)]
         for t in range(PACK):
-            pick_overlap(TANH, t, picked)
+            pick_overlap(LIN, t, picked[t])
 
-        h_sin = tile([P, PACK, S], F32, "h_sin", tag="h_b")
+        h_sin = tile([P, PACK, S], F32, "h_sin", tag="h_a")
         sin_work = tile([P, 2, S], F32, "sin_work", tag="xb")
         for t in range(PACK):
             acc = first_product(t, lambda a: w1_w[:, a, P * t:P * (t + 1)].bitcast(E4M3),
@@ -196,65 +231,48 @@ def tile_list_dome_seam_page_kernel(tc, tab_words, tab_scales, offs, w1, w2_word
             nc.scalar.activation(out=work, in_=work, func=ACT.Square)
             nc.scalar.activation(out=work, in_=work, func=ACT.Square, scale=-2.0, bias=one[:])
             nc.scalar.activation(out=h_sin[:, t, :], in_=work, func=ACT.Identity, scale=-2.0, bias=one[:])
-        xi_tanh = round_x(TANH, picked)
-        w3_b0 = round_weight(w3_raw0, "w3_b0", "woven", 3)
-        w3_b1 = round_weight(w3_raw1, "w3_b1", "picked", 1)
-        for t in range(PACK):
-            scatter(SIN, t, h_sin)
-        quantize(xi_tanh[:], x_w[TANH][:], x_s[TANH][:])
-        w4_s = tile([P, H], U8, "w4_s")
-        nc.vector.tensor_copy(out=w4_s[:].rearrange("p (g t m) -> p g t m", g=3, t=PACK),
-                              in_=w4s_raw[:].rearrange("p (g m t) -> p g t m", g=3, t=PACK))
-        w3_w = tile([P, 2, R], U32, "w3_w")
-        w3_s = tile([P, 2, R], U8, "w3_s")
-        quantize(w3_b0[:], w3_w[:, 0, :], w3_s[:, 0, :])
-        quantize(w3_b1[:], w3_w[:, 1, :], w3_s[:, 1, :])
-        picked = tile([P, PACK, M], F32, "picked_sin", tag="picked")
-        for t in range(PACK):
-            pick_overlap(SIN, t, picked)
-
-        h_lin = tile([P, PACK, S], F32, "h_lin", tag="h_a")
-        for t in range(PACK):
-            acc = first_product(t, lambda a: w3_w[:, a, P * t:P * (t + 1)].bitcast(E4M3),
-                                lambda a: w3_s[:, a, P * t:P * (t + 1)])
-            nc.scalar.copy(out=h_lin[:, t, :], in_=acc[:])
-        xi_sin = round_x(SIN, picked)
+        xi_lin = weave_x(LIN, round_x(LIN, picked))
         w4_w = [tile([P, H], U32, "w4_w%d" % a) for a in range(3)]
         for a in BANK_ORDER:
             nc.scalar.copy(out=w4_w[a][:].rearrange("p (g t c i) -> p g c t i", g=3, t=PACK, i=4),
                            in_=w4_raw[a][:].rearrange("p (g c i t) -> p g c t i", g=3, t=PACK, i=4))
-        picked = tile([P, PACK, M], F32, "picked_lin", tag="picked")
-        scatter(LIN, 0, h_lin)
-        scatter(LIN, 1, h_lin)
-        pick_overlap(LIN, 0, picked)
-        scatter(LIN, 2, h_lin)
-        pick_overlap(LIN, 1, picked)
-        quantize(xi_sin[:], x_w[SIN][:], x_s[SIN][:])
-        pick_overlap(LIN, 2, picked)
-        scatter(LIN, 3, h_lin)
-        xb = tile([P, PACK - 1, M], BF16, "xb_lin", tag="xb")
+        picked = tile([P, PACK, M], F32, "picked_sin", tag="picked")
+        scatter(SIN, 0, h_sin)
+        scatter(SIN, 1, h_sin)
+        pick_overlap(SIN, 0, picked[:, 0, :])
+        scatter(SIN, 2, h_sin)
+        pick_overlap(SIN, 1, picked[:, 1, :])
+        quantize(xi_lin[:], x_w[LIN][:], x_s[LIN][:])
+        pick_overlap(SIN, 2, picked[:, 2, :])
+        scatter(SIN, 3, h_sin)
+        xb = tile([P, PACK - 1, M], BF16, "xb_sin", tag="xb")
         for t in range(PACK - 1):
-            nc.scalar.activation(out=xb[:, t, :], in_=picked[:, t, :], func=ACT.Abs, scale=gx_t[:, LIN, t:t + 1])
-        xi_lin = tile([P, M * PACK], BF16, "xi_lin", tag="last_x")
-        xi_view = xi_lin[:].rearrange("p (m t) -> p m t", t=PACK)
+            nc.scalar.activation(out=xb[:, t, :], in_=picked[:, t, :], func=ACT.Abs, scale=gx_t[:, SIN, t:t + 1])
+        xi_sin = tile([P, M * PACK], BF16, "xi_sin", tag="last_x")
+        xi_view = xi_sin[:].rearrange("p (m t) -> p m t", t=PACK)
         nc.scalar.copy(out=xi_view[:, :, 0:PACK - 1], in_=xb[:].rearrange("p t m -> p m t"))
 
         opposite = tile([P, PACK - 1, M], F32, "opposite", tag="h_a")
-        slots = [opposite[:, t, :] for t in range(PACK - 1)]
+        slot_of = {n: opposite[:, n, :] for n in range(PACK - 1)}
 
         def pick_opposite(n):
-            nc.vector.tensor_copy(slots[n % PACK], pages[n // PACK, n % PACK][:].indirect(idx4[:]))
+            nc.vector.tensor_copy(slot_of[n], pages[n // PACK, n % PACK][:].indirect(idx4[:]))
 
         pick_opposite(0)
-        pick_overlap(LIN, PACK - 1, picked)
+        pick_overlap(SIN, PACK - 1, picked[:, PACK - 1, :])
         nc.scalar.activation(out=xi_view[:, :, PACK - 1], in_=picked[:, PACK - 1, :], func=ACT.Abs,
-                             scale=gx_t[:, LIN, PACK - 1:PACK])
+                             scale=gx_t[:, SIN, PACK - 1:PACK])
         pick_opposite(1)
         pick_opposite(2)
-        quantize(xi_lin[:], x_w[LIN][:], x_s[LIN][:])
+        quantize(xi_sin[:], x_w[SIN][:], x_s[SIN][:])
         opposite_late = tile([P, M], F32, "opposite_late", tag="last_x")
-        slots.append(opposite_late[:])
+        slot_of[3] = opposite_late[:]
         pick_opposite(3)
+        picks_after = {}
+        for n in range(PACK, 3 * PACK):
+            back = 4 if n < 2 * PACK else 3
+            slot_of[n] = slot_of[n - back]
+            picks_after[n - back + 1] = n
 
         y_w = [tile([P, M], U32, "y_w%d" % g) for g in range(3)]
         y_s = tile([P, 3, M], U8, "y_s")
@@ -269,7 +287,7 @@ def tile_list_dome_seam_page_kernel(tc, tab_words, tab_scales, offs, w1, w2_word
             if g == 0:
                 y = tile([P, PACK, M], F32, "y0", tag="h_b")
             else:
-                y = tile([P, PACK, M], F32, "y%d" % g, tag="stage", bufs=2)
+                y = tile([P, PACK, M], F32, "y%d" % g, tag="stage", bufs=3)
             y_rows = out_0[g * GROUP:(g + 1) * GROUP, :].rearrange("(p t) m -> p t m", t=PACK)
             for t in range(PACK):
                 n = PACK * g + t
@@ -281,10 +299,10 @@ def tile_list_dome_seam_page_kernel(tc, tab_words, tab_scales, offs, w1, w2_word
                                         start=(a == BANK_ORDER[0]), stop=(a == BANK_ORDER[-1]))
                 halves = [slice(0, M // 2), slice(M // 2, M)] if n == 3 * PACK - 1 else [slice(0, M)]
                 for part in halves:
-                    nc.vector.scalar_tensor_tensor(out=y[:, t, part], in0=slots[t][:, part], scalar=gv_t[:, g, t:t + 1],
+                    nc.vector.scalar_tensor_tensor(out=y[:, t, part], in0=slot_of[n][:, part], scalar=gv_t[:, g, t:t + 1],
                                                    in1=acc[:, part], op0=ALU.mult, op1=ALU.add)
-                if 1 <= n and n + 3 < 3 * PACK:
-                    pick_opposite(n + 3)
+                if n in picks_after:
+                    pick_opposite(picks_after[n])
                 for part in halves:
                     nc.scalar.activation(out=y[:, t, part], in_=y[:, t, part], func=ACT.Sigmoid)
                 nc.sync.dma_start(out=y_rows[:, t, :], in_=y[:, t, :])

@@ -93,7 +93,7 @@ def tile_list_dome_seam_page_kernel(tc, tab_words, tab_scales, offs, w1, w2_word
         wgs_rows = wgs.rearrange("(q t) j -> q t j", t=PACK)
         wgs_first = tile([P, S], F32, "wgs_first")
         for q in range(QUADS):
-            nc.gpsimd.dma_start(out=wgs_first[32 * q:32 * q + 32, :], in_=wgs_rows[:, 0, :])
+            nc.sync.dma_start(out=wgs_first[32 * q:32 * q + 32, :], in_=wgs_rows[:, 0, :])
         pages = {}
         pages[TANH, 0] = load_page(TANH, 0)
         pages[TANH, 1] = load_page(TANH, 1)
@@ -108,6 +108,15 @@ def tile_list_dome_seam_page_kernel(tc, tab_words, tab_scales, offs, w1, w2_word
         idx3 = load_list(offs3, "idx3")
         gx_t = tile([P, 3, PACK], F32, "gx_t")
         nc.sync.dma_start(out=gx_t[:], in_=gx.rearrange("(a p t) -> p a t", a=3, t=PACK))
+        gv_t = tile([P, 3, PACK], F32, "gv_t")
+        nc.sync.dma_start(out=gv_t[:], in_=gv.rearrange("(a p t) -> p a t", a=3, t=PACK))
+        gv_nudge = tile([P, 3, PACK], F32, "gv_nudge")
+        nc.gpsimd.tensor_tensor(gv_nudge[:], gv_t[:], gv_t[:], ALU.mult)
+        nc.gpsimd.tensor_scalar(gv_nudge[:], gv_nudge[:], 2.0 ** -120, 2.0 ** -59, ALU.is_lt, ALU.mult)
+        gv_safe = tile([P, 3, PACK], F32, "gv_safe")
+        nc.gpsimd.tensor_tensor(gv_safe[:], gv_t[:], gv_nudge[:], ALU.add)
+        gv_inv = tile([P, 3, PACK], F32, "gv_inv")
+        nc.vector.reciprocal(gv_inv[:], gv_safe[:])
         w1_raw0 = load_weight(w1, 0, "w1_raw0")
         pages[LIN, 0] = load_page(LIN, 0)
 
@@ -180,8 +189,6 @@ def tile_list_dome_seam_page_kernel(tc, tab_words, tab_scales, offs, w1, w2_word
         load_w4(LIN)
         load_w4(SIN)
         idx4 = load_list(offs4, "idx4")
-        gv_t = tile([P, 3, PACK], F32, "gv_t")
-        nc.sync.dma_start(out=gv_t[:], in_=gv.rearrange("(a p t) -> p a t", a=3, t=PACK))
 
         for t, j0, j1 in tanh_parts:
             scatter(TANH, t, h_tanh, j0, j1)
@@ -268,55 +275,75 @@ def tile_list_dome_seam_page_kernel(tc, tab_words, tab_scales, offs, w1, w2_word
         opposite_late = tile([P, M], F32, "opposite_late", tag="last_x")
         slot_of[3] = opposite_late[:]
         pick_opposite(3)
-        picks_after = {}
-        for n in range(PACK, 3 * PACK):
-            back = 4 if n < 2 * PACK else 3
-            slot_of[n] = slot_of[n - back]
-            picks_after[n - back + 1] = n
 
         y_w = [tile([P, M], U32, "y_w%d" % g) for g in range(3)]
         y_s = tile([P, 3, M], U8, "y_s")
-        y_rounded = {}
+        y = [tile([P, PACK, M], F32, "y0", tag="h_b")]
+        y += [tile([P, PACK, M], F32, "y%d" % g, tag="stage", bufs=3) for g in (1, 2)]
+        y_b = [tile([P, M * PACK], BF16, "y_b%d" % g, tag="woven", bufs=3) for g in range(3)]
+        e_acc = {}
+
+        def second_product(n):
+            acc = psum.tile([P, M], F32, name="e_acc%d" % n, tag="bank%d" % ((4 + n) % 8))
+            cols = slice(P * n, P * (n + 1))
+            for a in BANK_ORDER:
+                nc.tensor.matmul_mx(out=acc[:], lhsT=w4_w[a][:, cols].bitcast(E4M3), lhsT_scale=w4_s[4 * a:P, cols],
+                                    rhs=x_w[a][:].bitcast(E4M3), rhs_scale=x_s[a][:],
+                                    start=(a == BANK_ORDER[0]), stop=(a == BANK_ORDER[-1]))
+            e_acc[n] = acc
+
+        def add_picked(t):
+            nc.vector.scalar_tensor_tensor(out=y[0][:, t, :], in0=slot_of[t], scalar=gv_t[:, 0, t:t + 1],
+                                           in1=e_acc[t][:], op0=ALU.mult, op1=ALU.add)
+
+        e_over_gv = {1: tile([P, PACK, M], F32, "e_over_gv1", tag="picked"),
+                     2: tile([P, PACK, M], F32, "e_over_gv2", tag="h_a")}
+
+        def divide_e(n):
+            g, t = divmod(n, PACK)
+            nc.scalar.activation(out=e_over_gv[g][:, t, :], in_=e_acc[n][:], func=ACT.Copy, scale=gv_inv[:, g, t:t + 1])
+
+        def pick_and_add(n):
+            g, t = divmod(n, PACK)
+            nc.vector.tensor_tensor(y[g][:, t, :], pages[g, t][:].indirect(idx4[:]), e_over_gv[g][:, t, :], ALU.add)
+
+        def sigmoid(n):
+            g, t = divmod(n, PACK)
+            scale = 1.0 if g == 0 else gv_safe[:, g, t:t + 1]
+            nc.scalar.activation(out=y[g][:, t, :], in_=y[g][:, t, :], func=ACT.Sigmoid, scale=scale)
+            rows = out_0[g * GROUP:(g + 1) * GROUP, :].rearrange("(p t) m -> p t m", t=PACK)
+            nc.sync.dma_start(out=rows[:, t, :], in_=y[g][:, t, :])
+
+        def round_y(engine_copy, g, m0, m1):
+            interleave(engine_copy, y_b[g][:, PACK * m0:PACK * m1], y[g][:, :, m0:m1])
 
         def finish_group(g, m0, m1):
-            quantize(y_rounded[g][:, PACK * m0:PACK * m1], y_w[g][:, m0:m1], y_s[:, g, m0:m1])
+            quantize(y_b[g][:, PACK * m0:PACK * m1], y_w[g][:, m0:m1], y_s[:, g, m0:m1])
             nc.sync.dma_start(out=out_1[g].rearrange("p m t -> p (m t)").bitcast(I32)[:, m0:m1],
                               in_=y_w[g][:, m0:m1].bitcast(I32))
 
-        for g in range(3):
-            if g == 0:
-                y = tile([P, PACK, M], F32, "y0", tag="h_b")
-            else:
-                y = tile([P, PACK, M], F32, "y%d" % g, tag="stage", bufs=3)
-            y_rows = out_0[g * GROUP:(g + 1) * GROUP, :].rearrange("(p t) m -> p t m", t=PACK)
-            for t in range(PACK):
-                n = PACK * g + t
-                acc = psum.tile([P, M], F32, name="e_acc%d" % n, tag="bank%d" % ((4 + n) % 8))
-                cols = slice(P * n, P * (n + 1))
-                for a in BANK_ORDER:
-                    nc.tensor.matmul_mx(out=acc[:], lhsT=w4_w[a][:, cols].bitcast(E4M3), lhsT_scale=w4_s[4 * a:P, cols],
-                                        rhs=x_w[a][:].bitcast(E4M3), rhs_scale=x_s[a][:],
-                                        start=(a == BANK_ORDER[0]), stop=(a == BANK_ORDER[-1]))
-                halves = [slice(0, M // 2), slice(M // 2, M)] if n == 3 * PACK - 1 else [slice(0, M)]
-                for part in halves:
-                    nc.vector.scalar_tensor_tensor(out=y[:, t, part], in0=slot_of[n][:, part], scalar=gv_t[:, g, t:t + 1],
-                                                   in1=acc[:, part], op0=ALU.mult, op1=ALU.add)
-                if n in picks_after:
-                    pick_opposite(picks_after[n])
-                for part in halves:
-                    nc.scalar.activation(out=y[:, t, part], in_=y[:, t, part], func=ACT.Sigmoid)
-                nc.sync.dma_start(out=y_rows[:, t, :], in_=y[:, t, :])
-                if (g, t) in ((1, 2), (2, 3)):
-                    finish_group(g - 1, 0, M)
-            y_rounded[g] = tile([P, M * PACK], BF16, "y_b%d" % g, tag="woven", bufs=3)
-            if g < 2:
-                interleave(nc.scalar.copy, y_rounded[g][:], y[:])
-            else:
-                for m0 in (0, M // 2):
-                    m1 = m0 + M // 2
-                    interleave(nc.vector.tensor_copy, y_rounded[g][:, PACK * m0:PACK * m1], y[:, :, m0:m1])
-                for m0 in (0, M // 2):
-                    finish_group(g, m0, m0 + M // 2)
+        for t in range(PACK):
+            second_product(t)
+            second_product(PACK + t)
+            add_picked(t)
+            divide_e(PACK + t)
+            sigmoid(t)
+        for n in range(PACK, 2 * PACK):
+            second_product(PACK + n)
+            pick_and_add(n)
+            divide_e(PACK + n)
+            sigmoid(n)
+        round_y(nc.scalar.copy, 0, 0, M)
+        for n in range(2 * PACK, 3 * PACK):
+            pick_and_add(n)
+            sigmoid(n)
+        round_y(nc.vector.tensor_copy, 1, 0, M)
+        finish_group(0, 0, M)
+        round_y(nc.vector.tensor_copy, 2, 0, M // 2)
+        round_y(nc.scalar.copy, 2, M // 2, M)
+        finish_group(1, 0, M)
+        finish_group(2, 0, M // 2)
+        finish_group(2, M // 2, M)
         for q in range(QUADS):
             engine = nc.sync if q < 2 else nc.scalar
             engine.dma_start(out=out_2[:, 4 * q:4 * q + 4, :].rearrange("g q m -> q g m").bitcast(I32),

@@ -91,16 +91,20 @@ def tile_list_dome_seam_page_kernel(tc, tab_words, tab_scales, offs, w1, w2_word
         nc.sync.dma_start(out=tab_w[1][:].bitcast(I32), in_=tab_words[1].rearrange("p c i -> p (c i)").bitcast(I32))
         idx2 = load_list(offs2, "idx2")
         wgs_rows = wgs.rearrange("(q t) j -> q t j", t=PACK)
-        wgs_first = tile([P, S], F32, "wgs_first")
-        for q in range(QUADS):
-            nc.sync.dma_start(out=wgs_first[32 * q:32 * q + 32, :], in_=wgs_rows[:, 0, :])
+        wgs_of = []
+
+        def load_wgs(t0, t1):
+            part = tile([P, t1 - t0, S], F32, "wgs%d" % t0)
+            for q in range(QUADS):
+                nc.sync.dma_start(out=part[32 * q:32 * q + 32, :, :], in_=wgs_rows[:, t0:t1, :])
+            wgs_of.extend(part[:, t, :] for t in range(t1 - t0))
+
         pages = {}
+        load_wgs(0, 1)
         pages[TANH, 0] = load_page(TANH, 0)
+        load_wgs(1, 2)
         pages[TANH, 1] = load_page(TANH, 1)
-        wgs_rest = tile([P, PACK - 1, S], F32, "wgs_rest")
-        for q in range(QUADS):
-            nc.sync.dma_start(out=wgs_rest[32 * q:32 * q + 32, :, :], in_=wgs_rows[:, 1:PACK, :])
-        wgs_of = [wgs_first[:]] + [wgs_rest[:, t, :] for t in range(PACK - 1)]
+        load_wgs(2, PACK)
         pages[TANH, 2] = load_page(TANH, 2)
         w3_raw0 = load_weight(w3, 0, "w3_raw0")
         pages[TANH, 3] = load_page(TANH, 3)
@@ -259,8 +263,9 @@ def tile_list_dome_seam_page_kernel(tc, tab_words, tab_scales, offs, w1, w2_word
         xi_view = xi_sin[:].rearrange("p (m t) -> p m t", t=PACK)
         nc.scalar.copy(out=xi_view[:, :, 0:PACK - 1], in_=xb[:].rearrange("p t m -> p m t"))
 
-        opposite = tile([P, PACK - 1, M], F32, "opposite", tag="h_a")
-        slot_of = {n: opposite[:, n, :] for n in range(PACK - 1)}
+        opposite_first = tile([P, M], F32, "opposite_first", tag="h_a")
+        opposite_next = tile([P, 2, M], F32, "opposite_next", tag="xb")
+        slot_of = {0: opposite_first[:], 1: opposite_next[:, 0, :], 2: opposite_next[:, 1, :]}
 
         def pick_opposite(n):
             nc.vector.tensor_copy(slot_of[n], pages[n // PACK, n % PACK][:].indirect(idx4[:]))
@@ -296,8 +301,8 @@ def tile_list_dome_seam_page_kernel(tc, tab_words, tab_scales, offs, w1, w2_word
             nc.vector.scalar_tensor_tensor(out=y[0][:, t, :], in0=slot_of[t], scalar=gv_t[:, 0, t:t + 1],
                                            in1=e_acc[t][:], op0=ALU.mult, op1=ALU.add)
 
-        e_over_gv = {1: tile([P, PACK, M], F32, "e_over_gv1", tag="picked"),
-                     2: tile([P, PACK, M], F32, "e_over_gv2", tag="h_a")}
+        e_over_gv = {1: tile([P, PACK, M], F32, "e_over_gv1", tag="h_a"),
+                     2: tile([P, PACK, M], F32, "e_over_gv2", tag="picked")}
 
         def divide_e(n):
             g, t = divmod(n, PACK)
@@ -326,22 +331,24 @@ def tile_list_dome_seam_page_kernel(tc, tab_words, tab_scales, offs, w1, w2_word
             second_product(t)
             second_product(PACK + t)
             add_picked(t)
-            divide_e(PACK + t)
             sigmoid(t)
+            divide_e(PACK + t)
         for n in range(PACK, 2 * PACK):
             second_product(PACK + n)
             pick_and_add(n)
             divide_e(PACK + n)
             sigmoid(n)
-        round_y(nc.scalar.copy, 0, 0, M)
+            if n == PACK + 1:
+                round_y(nc.vector.tensor_copy, 0, 0, M)
+            if n == PACK + 2:
+                finish_group(0, 0, M)
+        round_y(nc.scalar.copy, 1, 0, M)
         for n in range(2 * PACK, 3 * PACK):
             pick_and_add(n)
             sigmoid(n)
-        round_y(nc.vector.tensor_copy, 1, 0, M)
-        finish_group(0, 0, M)
+        finish_group(1, 0, M)
         round_y(nc.vector.tensor_copy, 2, 0, M // 2)
         round_y(nc.scalar.copy, 2, M // 2, M)
-        finish_group(1, 0, M)
         finish_group(2, 0, M // 2)
         finish_group(2, M // 2, M)
         for q in range(QUADS):

import math
from contextlib import ExitStack

import concourse.mybir as mybir

K, R, H, T, S, T2, M = 1024, 512, 1536, 2048, 512, 1024, 512
FLOPS = 2 * 3 * K * R * S + 2 * H * H * M

F32 = mybir.dt.float32
BF16 = mybir.dt.bfloat16
I32 = mybir.dt.int32
U32 = mybir.dt.uint32
U16 = mybir.dt.uint16
U8 = mybir.dt.uint8
E4M3 = mybir.dt.float8_e4m3fn_x4
E2M1 = mybir.dt.float4_e2m1fn_x4
ACT = mybir.ActivationFunctionType
ALU = mybir.AluOpType

P = 128
PACK = 4
GROUP = P * PACK
QUADS = 4
SIN, TANH, LIN = 0, 1, 2
BANK_ORDER = (TANH, LIN, SIN)


def tile_list_dome_seam_page_kernel(tc, tab_words, tab_scales, offs, w1, w2_words, w2_scales, w3, page0, wgs,
                                              offs2, offs3, gx, w4_words, w4_scales, offs4, gv, out_0, out_1, out_2):
    nc = tc.nc
    with ExitStack() as ctx:
        lists = ctx.enter_context(tc.tile_pool(name="lists", bufs=1))
        sb = ctx.enter_context(tc.tile_pool(name="sb", bufs=1))
        psum = ctx.enter_context(tc.psum_pool(name="psum", bufs=1))

        def tile(shape, dtype, name, tag=None, bufs=1):
            return sb.tile(shape, dtype, name=name, tag=tag or name, bufs=bufs, align_bytes=64)

        def load_list(src, name):
            t = lists.tile([P, S // 16], U16, name=name)
            nc.sync.dma_start(t[:], src)
            return t

        def load_page(bank, t):
            pg = tile([P, T2], F32, "page_%d_%d" % (bank, t))
            rows = page0[bank * GROUP:(bank + 1) * GROUP, :].rearrange("(p t) c -> p t c", t=PACK)
            nc.sync.dma_start(out=pg[:], in_=rows[:, t, :])
            return pg

        def load_scale_rows(engine, dst, src):
            for q in range(QUADS):
                engine.dma_start(out=dst[32 * q:32 * q + 4, :, :].bitcast(I32),
                                 in_=src[:, 4 * q:4 * q + 4, :].rearrange("a q c -> q a c").bitcast(I32))

        def load_weight(w, a, name):
            raw = tile([P, PACK, R], F32, name, tag="stage", bufs=3)
            nc.sync.dma_start(out=raw[:], in_=w[a * GROUP:(a + 1) * GROUP, :].rearrange("(p j) c -> p j c", j=PACK))
            return raw

        def round_weight(raw, name, tag, bufs):
            wb = tile([P, R * PACK], BF16, name, tag=tag, bufs=bufs)
            nc.scalar.copy(out=wb[:].rearrange("p (t m j) -> p m t j", t=PACK, j=PACK),
                           in_=raw[:].rearrange("p j (m t) -> p m t j", t=PACK))
            return wb

        def quantize(src, codes, scales):
            nc.vector.quantize_mx(out=codes.bitcast(E4M3), scales=scales, in_=src)

        def interleave(engine_copy, dst, src):
            engine_copy(out=dst.rearrange("p (c i t) -> p c t i", i=4, t=PACK),
                        in_=src.rearrange("p t (c i) -> p c t i", i=4))

        tab_s = tile([P, 2, T], U8, "tab_s")
        nc.vector.memset(tab_s[:].rearrange("p a c -> p (a c)").bitcast(I32), 0)
        w2s_raw = tile([P, 2, R], U8, "w2s_raw")
        nc.gpsimd.memset(w2s_raw[:].rearrange("p a c -> p (a c)").bitcast(I32), 0)
        load_scale_rows(nc.sync, w2s_raw, w2_scales)
        w4s_raw = tile([P, H], U8, "w4s_raw")
        nc.gpsimd.memset(w4s_raw[:].bitcast(I32), 0)
        one = tile([P, 1], F32, "one")
        nc.gpsimd.memset(one[:], 1.0)
        eighth_pi = tile([P, 1], F32, "eighth_pi")
        nc.gpsimd.tensor_scalar(eighth_pi[:], one[:], math.pi / 8, 0.0, ALU.mult, ALU.add)

        tab_w = [tile([P, T], U32, "tab_w%d" % a) for a in range(2)]
        nc.sync.dma_start(out=tab_w[0][:].bitcast(I32), in_=tab_words[0].rearrange("p c i -> p (c i)").bitcast(I32))
        idx = load_list(offs, "idx")
        load_scale_rows(nc.sync, tab_s, tab_scales)
        w2_raw = tile([P, 2, 2 * R], U8, "w2_raw")
        nc.sync.dma_start(out=w2_raw[:].bitcast(I32), in_=w2_words.rearrange("a p c -> p a c").bitcast(I32))
        nc.sync.dma_start(out=tab_w[1][:].bitcast(I32), in_=tab_words[1].rearrange("p c i -> p (c i)").bitcast(I32))
        idx2 = load_list(offs2, "idx2")
        wgs_rows = wgs.rearrange("(q t) j -> q t j", t=PACK)
        wgs_of = []

        def load_wgs(t0, t1):
            part = tile([P, t1 - t0, S], F32, "wgs%d" % t0)
            for q in range(QUADS):
                nc.sync.dma_start(out=part[32 * q:32 * q + 32, :, :], in_=wgs_rows[:, t0:t1, :])
            wgs_of.extend(part[:, t, :] for t in range(t1 - t0))

        pages = {}
        load_wgs(0, 1)
        pages[TANH, 0] = load_page(TANH, 0)
        load_wgs(1, 2)
        pages[TANH, 1] = load_page(TANH, 1)
        load_wgs(2, PACK)
        pages[TANH, 2] = load_page(TANH, 2)
        w3_raw0 = load_weight(w3, 0, "w3_raw0")
        pages[TANH, 3] = load_page(TANH, 3)
        w3_raw1 = load_weight(w3, 1, "w3_raw1")
        idx3 = load_list(offs3, "idx3")
        gx_t = tile([P, 3, PACK], F32, "gx_t")
        nc.sync.dma_start(out=gx_t[:], in_=gx.rearrange("(a p t) -> p a t", a=3, t=PACK))
        gv_t = tile([P, 3, PACK], F32, "gv_t")
        nc.sync.dma_start(out=gv_t[:], in_=gv.rearrange("(a p t) -> p a t", a=3, t=PACK))
        gv_nudge = tile([P, 3, PACK], F32, "gv_nudge")
        nc.gpsimd.tensor_tensor(gv_nudge[:], gv_t[:], gv_t[:], ALU.mult)
        nc.gpsimd.tensor_scalar(gv_nudge[:], gv_nudge[:], 2.0 ** -120, 2.0 ** -59, ALU.is_lt, ALU.mult)
        gv_safe = tile([P, 3, PACK], F32, "gv_safe")
        nc.gpsimd.tensor_tensor(gv_safe[:], gv_t[:], gv_nudge[:], ALU.add)
        gv_inv = tile([P, 3, PACK], F32, "gv_inv")
        nc.vector.reciprocal(gv_inv[:], gv_safe[:])
        w1_raw0 = load_weight(w1, 0, "w1_raw0")
        pages[LIN, 0] = load_page(LIN, 0)

        v_w = tile([P, 2, S], U32, "v_w")
        v_s = tile([P, 2, S], U8, "v_s")
        w2_s = tile([P, 2, R], U8, "w2_s")
        nc.vector.tensor_copy(out=w2_s[:].rearrange("p a (t m) -> p a t m", t=PACK),
                              in_=w2s_raw[:].rearrange("p a (m t) -> p a t m", t=PACK))
        nc.vector.tensor_copy(v_w[:, 0, :], tab_w[0][:].indirect(idx[:]))
        for a in range(2):
            nc.vector.tensor_copy(v_s[:, a, :], tab_s[:, a, :].indirect(idx[:]))
        for j0 in (0, S // 2):
            nc.vector.tensor_copy(v_w[:, 1, j0:j0 + S // 2], tab_w[1][:].indirect(idx[:, j0 // 16:(j0 + S // 2) // 16]))
        w2_w = tile([P, 2, 2 * R], U8, "w2_w")
        nc.scalar.copy(out=w2_w[:].bitcast(U16).rearrange("p a (t m) -> p a t m", t=PACK),
                       in_=w2_raw[:].bitcast(U16).rearrange("p a (m t) -> p a t m", t=PACK))

        def first_product(psum_bank, codes_of, scales_of, j0=0, j1=S):
            acc = psum.tile([P, j1 - j0], F32, name="h_acc", tag="bank%d" % psum_bank)
            for a in range(2):
                nc.tensor.matmul_mx(out=acc[:], lhsT=codes_of(a), lhsT_scale=scales_of(a),
                                    rhs=v_w[:, a, j0:j1].bitcast(E4M3), rhs_scale=v_s[:, a, j0:j1],
                                    start=(a == 0), stop=(a == 1))
            return acc

        def scatter(bank, t, h, j0=0, j1=S):
            nc.vector.tensor_tensor(pages[bank, t][:].indirect(idx2[:, j0 // 16:j1 // 16]), h[:, t, j0:j1],
                                    wgs_of[t][:, j0:j1], ALU.mult)

        def pick_overlap(bank, t, picked):
            nc.vector.tensor_copy(picked, pages[bank, t][:].indirect(idx3[:]))

        x_w = [tile([P, M], U32, "x_w%d" % a) for a in range(3)]
        x_s = [tile([P, M], U8, "x_s%d" % a) for a in range(3)]

        def round_x(bank, picked):
            xb = tile([P, PACK, M], BF16, "xb%d" % bank, tag="xb")
            for t in range(PACK):
                nc.scalar.activation(out=xb[:, t, :], in_=picked[t], func=ACT.Abs, scale=gx_t[:, bank, t:t + 1])
            return xb

        def weave_x(bank, xb):
            xi = tile([P, M * PACK], BF16, "xi%d" % bank, tag="woven", bufs=3)
            interleave(nc.scalar.copy, xi[:], xb[:])
            return xi

        h_tanh = tile([P, PACK, S], F32, "h_tanh", tag="h_a")
        tanh_parts = [(0, 0, S // 2), (0, S // 2, S)] + [(t, 0, S) for t in range(1, PACK)]
        for psum_bank, (t, j0, j1) in enumerate(tanh_parts):
            acc = first_product(psum_bank, lambda a: w2_w[:, a, 2 * P * t:2 * P * (t + 1)].bitcast(E2M1),
                                lambda a: w2_s[:, a, P * t:P * (t + 1)], j0, j1)
            nc.scalar.activation(out=h_tanh[:, t, j0:j1], in_=acc[:], func=ACT.Tanh)
        w3_b0 = round_weight(w3_raw0, "w3_b0", "woven", 3)
        w3_b1 = round_weight(w3_raw1, "w3_b1", "picked", 1)
        w1_raw1 = load_weight(w1, 1, "w1_raw1")
        pages[LIN, 1] = load_page(LIN, 1)
        pages[LIN, 2] = load_page(LIN, 2)
        for q in range(QUADS):
            nc.sync.dma_start(out=w4s_raw[32 * q:32 * q + 12, :].bitcast(I32),
                              in_=w4_scales[:, 4 * q:4 * q + 4, :].bitcast(I32))
        pages[LIN, PACK - 1] = load_page(LIN, PACK - 1)
        for t in range(PACK):
            pages[SIN, t] = load_page(SIN, t)
        w4_raw = [tile([P, H], U32, "w4_raw%d" % a) for a in range(3)]

        def load_w4(a):
            nc.sync.dma_start(out=w4_raw[a][:].bitcast(I32), in_=w4_words[a].rearrange("p c i -> p (c i)").bitcast(I32))

        load_w4(TANH)
        load_w4(LIN)
        load_w4(SIN)
        idx4 = load_list(offs4, "idx4")

        for t, j0, j1 in tanh_parts:
            scatter(TANH, t, h_tanh, j0, j1)
        picked_early = tile([P, 2, M], F32, "picked_tanh_early", tag="h_a")
        for t in range(2):
            pick_overlap(TANH, t, picked_early[:, t, :])
        w3_w = tile([P, 2, R], U32, "w3_w")
        w3_s = tile([P, 2, R], U8, "w3_s")
        quantize(w3_b0[:], w3_w[:, 0, :], w3_s[:, 0, :])
        quantize(w3_b1[:], w3_w[:, 1, :], w3_s[:, 1, :])
        picked_late = tile([P, 2, M], F32, "picked_tanh_late", tag="picked")
        picked = [picked_early[:, 0, :], picked_early[:, 1, :], picked_late[:, 0, :], picked_late[:, 1, :]]
        for t in range(2, PACK):
            pick_overlap(TANH, t, picked[t])

        h_lin = tile([P, PACK, S], F32, "h_lin", tag="h_b")
        for t in range(PACK):
            acc = first_product(t, lambda a: w3_w[:, a, P * t:P * (t + 1)].bitcast(E4M3),
                                lambda a: w3_s[:, a, P * t:P * (t + 1)])
            nc.scalar.copy(out=h_lin[:, t, :], in_=acc[:])
        w1_b0 = round_weight(w1_raw0, "w1_b0", "woven", 3)
        xb_tanh = round_x(TANH, picked)
        w1_b1 = round_weight(w1_raw1, "w1_b1", "picked", 1)
        xi_tanh = weave_x(TANH, xb_tanh)
        for t in range(PACK):
            scatter(LIN, t, h_lin)
        w1_w = tile([P, 2, R], U32, "w1_w")
        w1_s = tile([P, 2, R], U8, "w1_s")
        quantize(w1_b0[:], w1_w[:, 0, :], w1_s[:, 0, :])
        quantize(w1_b1[:], w1_w[:, 1, :], w1_s[:, 1, :])
        quantize(xi_tanh[:], x_w[TANH][:], x_s[TANH][:])
        w4_s = tile([P, H], U8, "w4_s")
        nc.vector.tensor_copy(out=w4_s[:].rearrange("p (g t m) -> p g t m", g=3, t=PACK),
                              in_=w4s_raw[:].rearrange("p (g m t) -> p g t m", g=3, t=PACK))
        picked_lin = tile([P, PACK, M], F32, "picked_lin", tag="picked")
        picked = [picked_lin[:, t, :] for t in range(PACK)]
        for t in range(PACK):
            pick_overlap(LIN, t, picked[t])

        h_sin = tile([P, PACK, S], F32, "h_sin", tag="h_a")
        sin_work = tile([P, 2, S], F32, "sin_work", tag="xb")
        for t in range(PACK):
            acc = first_product(t, lambda a: w1_w[:, a, P * t:P * (t + 1)].bitcast(E4M3),
                                lambda a: w1_s[:, a, P * t:P * (t + 1)])
            work = sin_work[:, t, :] if t < 2 else h_sin[:, t, :]
            nc.scalar.activation(out=work, in_=acc[:], func=ACT.Sin, scale=0.25, bias=eighth_pi[:])
            nc.scalar.activation(out=work, in_=work, func=ACT.Square)
            nc.scalar.activation(out=work, in_=work, func=ACT.Square, scale=-2.0, bias=one[:])
            nc.scalar.activation(out=h_sin[:, t, :], in_=work, func=ACT.Identity, scale=-2.0, bias=one[:])
        xi_lin = weave_x(LIN, round_x(LIN, picked))
        w4_w = [tile([P, H], U32, "w4_w%d" % a) for a in range(3)]
        for a in BANK_ORDER:
            nc.scalar.copy(out=w4_w[a][:].rearrange("p (g t c i) -> p g c t i", g=3, t=PACK, i=4),
                           in_=w4_raw[a][:].rearrange("p (g c i t) -> p g c t i", g=3, t=PACK, i=4))
        picked = tile([P, PACK, M], F32, "picked_sin", tag="picked")
        scatter(SIN, 0, h_sin)
        scatter(SIN, 1, h_sin)
        pick_overlap(SIN, 0, picked[:, 0, :])
        scatter(SIN, 2, h_sin)
        pick_overlap(SIN, 1, picked[:, 1, :])
        quantize(xi_lin[:], x_w[LIN][:], x_s[LIN][:])
        pick_overlap(SIN, 2, picked[:, 2, :])
        scatter(SIN, 3, h_sin)
        xb = tile([P, PACK - 1, M], BF16, "xb_sin", tag="xb")
        for t in range(PACK - 1):
            nc.scalar.activation(out=xb[:, t, :], in_=picked[:, t, :], func=ACT.Abs, scale=gx_t[:, SIN, t:t + 1])
        xi_sin = tile([P, M * PACK], BF16, "xi_sin", tag="last_x")
        xi_view = xi_sin[:].rearrange("p (m t) -> p m t", t=PACK)
        nc.scalar.copy(out=xi_view[:, :, 0:PACK - 1], in_=xb[:].rearrange("p t m -> p m t"))

        opposite_first = tile([P, M], F32, "opposite_first", tag="h_a")
        opposite_next = tile([P, 2, M], F32, "opposite_next", tag="xb")
        slot_of = {0: opposite_first[:], 1: opposite_next[:, 0, :], 2: opposite_next[:, 1, :]}

        def pick_opposite(n):
            nc.vector.tensor_copy(slot_of[n], pages[n // PACK, n % PACK][:].indirect(idx4[:]))

        pick_opposite(0)
        pick_overlap(SIN, PACK - 1, picked[:, PACK - 1, :])
        nc.scalar.activation(out=xi_view[:, :, PACK - 1], in_=picked[:, PACK - 1, :], func=ACT.Abs,
                             scale=gx_t[:, SIN, PACK - 1:PACK])
        pick_opposite(1)
        pick_opposite(2)
        quantize(xi_sin[:], x_w[SIN][:], x_s[SIN][:])
        opposite_late = tile([P, M], F32, "opposite_late", tag="last_x")
        slot_of[3] = opposite_late[:]
        pick_opposite(3)

        y_w = [tile([P, M], U32, "y_w%d" % g) for g in range(3)]
        y_s = tile([P, 3, M], U8, "y_s")
        y = [tile([P, PACK, M], F32, "y0", tag="h_b")]
        y += [tile([P, PACK, M], F32, "y%d" % g, tag="stage", bufs=3) for g in (1, 2)]
        y_b = [tile([P, M * PACK], BF16, "y_b%d" % g, tag="woven", bufs=3) for g in range(3)]
        e_acc = {}

        def second_product(n):
            acc = psum.tile([P, M], F32, name="e_acc%d" % n, tag="bank%d" % ((4 + n) % 8))
            cols = slice(P * n, P * (n + 1))
            for a in BANK_ORDER:
                nc.tensor.matmul_mx(out=acc[:], lhsT=w4_w[a][:, cols].bitcast(E4M3), lhsT_scale=w4_s[4 * a:P, cols],
                                    rhs=x_w[a][:].bitcast(E4M3), rhs_scale=x_s[a][:],
                                    start=(a == BANK_ORDER[0]), stop=(a == BANK_ORDER[-1]))
            e_acc[n] = acc

        def add_picked(t):
            nc.vector.scalar_tensor_tensor(out=y[0][:, t, :], in0=slot_of[t], scalar=gv_t[:, 0, t:t + 1],
                                           in1=e_acc[t][:], op0=ALU.mult, op1=ALU.add)

        e_over_gv = {1: tile([P, PACK, M], F32, "e_over_gv1", tag="h_a"),
                     2: tile([P, PACK, M], F32, "e_over_gv2", tag="picked")}

        def divide_e(n):
            g, t = divmod(n, PACK)
            nc.scalar.activation(out=e_over_gv[g][:, t, :], in_=e_acc[n][:], func=ACT.Copy, scale=gv_inv[:, g, t:t + 1])

        def pick_and_add(n):
            g, t = divmod(n, PACK)
            nc.vector.tensor_tensor(y[g][:, t, :], pages[g, t][:].indirect(idx4[:]), e_over_gv[g][:, t, :], ALU.add)

        def sigmoid(n):
            g, t = divmod(n, PACK)
            scale = 1.0 if g == 0 else gv_safe[:, g, t:t + 1]
            nc.scalar.activation(out=y[g][:, t, :], in_=y[g][:, t, :], func=ACT.Sigmoid, scale=scale)
            rows = out_0[g * GROUP:(g + 1) * GROUP, :].rearrange("(p t) m -> p t m", t=PACK)
            nc.sync.dma_start(out=rows[:, t, :], in_=y[g][:, t, :])

        def round_y(engine_copy, g, m0, m1):
            interleave(engine_copy, y_b[g][:, PACK * m0:PACK * m1], y[g][:, :, m0:m1])

        def finish_group(g, m0, m1):
            quantize(y_b[g][:, PACK * m0:PACK * m1], y_w[g][:, m0:m1], y_s[:, g, m0:m1])
            nc.sync.dma_start(out=out_1[g].rearrange("p m t -> p (m t)").bitcast(I32)[:, m0:m1],
                              in_=y_w[g][:, m0:m1].bitcast(I32))

        for t in range(PACK):
            second_product(t)
            second_product(PACK + t)
            add_picked(t)
            sigmoid(t)
            divide_e(PACK + t)
        for n in range(PACK, 2 * PACK):
            second_product(PACK + n)
            pick_and_add(n)
            divide_e(PACK + n)
            sigmoid(n)
            if n == PACK + 1:
                round_y(nc.vector.tensor_copy, 0, 0, M)
            if n == PACK + 2:
                finish_group(0, 0, M)
        round_y(nc.scalar.copy, 1, 0, M)
        for n in range(2 * PACK, 3 * PACK):
            pick_and_add(n)
            sigmoid(n)
        finish_group(1, 0, M)
        round_y(nc.vector.tensor_copy, 2, 0, M // 2)
        round_y(nc.scalar.copy, 2, M // 2, M)
        finish_group(2, 0, M // 2)
        finish_group(2, M // 2, M)
        for q in range(QUADS):
            engine = nc.sync if q < 2 else nc.scalar
            engine.dma_start(out=out_2[:, 4 * q:4 * q + 4, :].rearrange("g q m -> q g m").bitcast(I32),
                             in_=y_s[32 * q:32 * q + 4, :, :].bitcast(I32))
